import numpy as np
import ml_dtypes


def mxq(x, axis, fmt="e4m3"):
    dtype, down = {"e4m3": (ml_dtypes.float8_e4m3fn, 7), "e5m2": (ml_dtypes.float8_e5m2, 14)}[fmt]
    v = np.moveaxis(np.asarray(x, np.float32).astype(ml_dtypes.bfloat16).astype(np.float64), axis, -1)
    blocks = v.reshape(v.shape[:-1] + (-1, 32))
    amax = np.abs(blocks).max(-1, keepdims=True)
    byte = np.maximum(np.where(amax > 0, np.frexp(amax)[1] - 1 + 127, 0) - down, 1)
    scale = np.exp2(byte - 127.0)
    codes = (blocks / scale).astype(np.float32).astype(dtype).astype(np.float64)
    return np.moveaxis((codes * scale).reshape(v.shape), -1, axis)


WIDE = False


def mx_kscale(k):
    if not WIDE:
        return np.ones(k)
    levels = np.array([10, -10, 5, -5, 0])
    if k % 512:
        return np.exp2(np.random.permutation(np.resize(levels, k // 32))).repeat(32)
    a = np.empty((k // 512, 16))
    for p in range(k // 512):
        a[p, :8] = np.random.permutation(np.resize(levels, 8))
        for g in range(8):
            far = levels[np.abs(levels - a[p, g]) >= 10]
            a[p, g + 8] = far[np.random.randint(len(far))]
    return np.exp2(a.ravel()).repeat(32)


def f64(x):
    return np.asarray(x).astype(np.float64)


def striped(idx):
    return np.tile(idx.reshape(-1, 16).T, (8, 1)).astype(np.uint16)


def unstriped(offs):
    return offs[:16].T.reshape(-1).astype(np.int64)


def striped8(idx):
    return np.concatenate([x.reshape(-1, 16).T for x in idx]).astype(np.uint16)


def runs(offs, k):
    lists = np.stack([offs[16 * r : 16 * r + 16].T.reshape(-1) for r in range(8)]).astype(np.int64)
    return lists[np.arange(k) % 512 // 64]


def pack_weight(w):
    k, n = w.shape
    w = f64(np.asarray(w, np.float32).astype(ml_dtypes.bfloat16)).reshape(k // 32, 32, n)
    amax = np.abs(w).max(1)
    byte = np.clip(np.where(amax > 0, np.frexp(amax)[1] - 1 + 127 - 7, 1), 1, 254)
    scaled = (w * np.exp2(127.0 - byte)[:, None, :]).reshape(k, n).astype(np.float32)
    words = np.ascontiguousarray(scaled.reshape(k // 512, 128, 4, n).transpose(0, 1, 3, 2)).astype(ml_dtypes.float8_e4m3fn).view(np.uint8)
    return words, np.ascontiguousarray(byte.astype(np.uint8).reshape(k // 512, 16, n))


def unpack_weight(words, scales):
    g, p, n, _ = words.shape
    vals = np.ascontiguousarray(words).view(ml_dtypes.float8_e4m3fn).astype(np.float64) * np.repeat(np.exp2(scales.astype(np.float64) - 127.0), 8, axis=1)[..., None]
    return vals.transpose(0, 1, 3, 2).reshape(g * 512, n)


def relu(v):
    return np.maximum(v, 0.0)


def sigmoid(v):
    return 1.0 / (1.0 + np.exp(-np.maximum(v, -700.0)))

def planes(y):
    n, m = y.shape
    v = y.astype(np.float32).astype(ml_dtypes.bfloat16).astype(np.float64).reshape(n // 32, 32, m)
    top = np.abs(v).max(1)
    byte = np.clip(np.where(top > 0, np.frexp(top)[1] - 1 + 127 - 7, 1), 1, 254)
    codes = (v * np.exp2(127.0 - byte)[:, None, :]).reshape(n, m).astype(np.float32).astype(ml_dtypes.float8_e4m3fn).view(np.uint8)
    words = codes.reshape(n // 512, 128, 4, m).transpose(0, 1, 3, 2)
    return np.ascontiguousarray(words), np.ascontiguousarray(byte.astype(np.uint8).reshape(n // 512, 16, m))


K, T, S, G, H, C = 512, 1024, 512, 2048, 512, 512


def setup_inputs():
    n = np.random.standard_normal
    s = mx_kscale(K)[:, None]
    packed_xT = pack_weight(n((K, T)) * s)
    packed_dT = pack_weight(n((K, G)) / s)
    return {
        "x_words": packed_xT[0],
        "x_scales": packed_xT[1],
        "d_words": packed_dT[0],
        "d_scales": packed_dT[1],
        "gs": (np.random.uniform(0.5, 1.5, (K, 1)) / s).astype(np.float32),
        "offs": striped(np.random.permutation(T)[:S]),
        "k1": striped8(np.random.randint(0, G, (8, H))),
        "n1": striped8(np.stack([np.random.permutation(S) for _ in range(8)])),
        "n2": striped8(np.stack([np.random.permutation(S) for _ in range(8)])),
        "cand": striped(np.random.permutation(T)[:C]),
        "two": striped(np.random.permutation(T)[:S]),
        "k2": striped8(np.random.randint(0, G, (8, H))),
        "n3": striped8(np.stack([np.random.permutation(S) for _ in range(8)])),
        "n4": striped8(np.stack([np.random.permutation(S) for _ in range(8)])),
    }


def reference(x_words, x_scales, d_words, d_scales, gs, offs, k1, n1, n2, cand, two, k2, n3, n4):
    x_cand = unpack_weight(x_words, x_scales)[:, unstriped(cand)]
    d_k1 = unpack_weight(d_words, d_scales)[np.arange(K)[:, None], runs(k1, K)]
    xq = unpack_weight(x_words, x_scales)[:, unstriped(offs)]
    h = 0.0625 * (d_k1.T @ xq)
    pa = h - (h[np.arange(H)[:, None], runs(n1, H)])
    pb = h[np.arange(H)[:, None], runs(n2, H)] - h
    z = f64(gs) * (relu(np.minimum(pa, pb)) - (relu(-1.0 * np.maximum(pa, pb))))
    a = 0.0625 * ((x_cand.T @ mxq(z, 0, "e4m3")))
    d_k2 = unpack_weight(d_words, d_scales)[np.arange(K)[:, None], runs(k2, K)]
    x_two = unpack_weight(x_words, x_scales)[:, unstriped(two)]
    b = 0.0625 * (d_k2.T @ x_two)
    out_0 = a + (sigmoid(b[np.arange(H)[:, None], runs(n4, H)] - b)) * (a[np.arange(C)[:, None], runs(n3, C)] - a)
    return (out_0,) + planes(out_0)

@@ -1,0 +1,257 @@
+from contextlib import ExitStack
+
+import concourse.mybir as mybir
+from concourse.masks import make_identity
+
+K, T, S, G = 512, 1024, 512, 2048
+FLOPS = 3 * 2 * 512 * 512 * 512
+
+F32 = mybir.dt.float32
+BF16 = mybir.dt.bfloat16
+I32 = mybir.dt.int32
+U32 = mybir.dt.uint32
+U16 = mybir.dt.uint16
+U8 = mybir.dt.uint8
+FP8X4 = mybir.dt.float8_e4m3fn_x4
+ALU = mybir.AluOpType
+ACT = mybir.ActivationFunctionType
+
+P = 128
+PACK = 4
+HALF = S // 2
+SIXTEENTH = 0.0625
+
+
+def tile_picked_pqcjpullbminmod_none_po_kernel(
+    tc, x_words, x_scales, d_words, d_scales, gs, offs, k1, n1, n2, cand, two, k2, n3, n4, out_0, out_1, out_2
+):
+    nc = tc.nc
+    with ExitStack() as ctx:
+        lists = ctx.enter_context(tc.tile_pool(name="lists", bufs=1))
+        sb = ctx.enter_context(tc.tile_pool(name="sb", bufs=1))
+        ps = ctx.enter_context(tc.psum_pool(name="ps", bufs=1))
+
+        def new(name, shape, dtype, tag=""):
+            return sb.tile(shape, dtype, name=name, tag=tag or name, align_bytes=64)
+
+        def load_list(name, src):
+            tile = lists.tile([P, S // 16], U16, name=name)
+            nc.sync.dma_start(tile[:], src)
+            return tile
+
+        def half_cols(hf):
+            return slice(hf * HALF, (hf + 1) * HALF)
+
+        def half_list(lst, hf):
+            return lst[:, hf * HALF // 16 : (hf + 1) * HALF // 16]
+
+        xw = new("xw", [P, T], U32)
+        dw = new("dw", [P, G], U32)
+        xs = new("xs", [P, T], U8)
+        ds = new("ds", [P, G], U8)
+        nc.vector.memset(ds[:].bitcast(I32), 0)
+        nc.gpsimd.memset(xs[:].bitcast(I32), 0)
+
+        k1_l = load_list("k1_l", k1)
+        ds32 = ds[:].bitcast(I32)
+        d_rows = d_scales[0].bitcast(I32)
+        for e in range(2):
+            nc.sync.dma_start(ds32[e:P:16, :], d_rows[e:16:2, :])
+        offs_l = load_list("offs_l", offs)
+        nc.sync.dma_start(xw[:].bitcast(I32), x_words[0].rearrange("p n r -> p (n r)").bitcast(I32))
+        xs32 = xs[:].bitcast(I32)
+        x_rows = x_scales[0].bitcast(I32)
+        for q in range(4):
+            nc.scalar.dma_start(xs32[32 * q : 32 * q + 4, :], x_rows[4 * q : 4 * q + 4, :])
+        nc.sync.dma_start(dw[:].bitcast(I32), d_words[0].rearrange("p n r -> p (n r)").bitcast(I32))
+        gain = new("gain", [P, PACK], F32)
+        nc.scalar.dma_start(gain[:], gs.rearrange("(p t) o -> p (t o)", t=PACK))
+        k2_l = load_list("k2_l", k2)
+        n1_l = load_list("n1_l", n1)
+        n2_l = load_list("n2_l", n2)
+        two_l = load_list("two_l", two)
+        cand_l = load_list("cand_l", cand)
+        n4_l = load_list("n4_l", n4)
+        n3_l = load_list("n3_l", n3)
+
+        ident = new("ident", [P, P], F32)
+        make_identity(nc, ident[:])
+        gain16 = new("gain16", [P, PACK], F32)
+        nc.scalar.activation(gain16[:], gain[:], ACT.Copy, scale=SIXTEENTH)
+
+        def pick(name, table, lst, dtype, tag=""):
+            picked = new(name, [P, S], dtype, tag)
+            nc.vector.tensor_copy(picked[:], table[:].indirect(lst[:]))
+            return picked
+
+        def deal_words(name, picked):
+            dealt = new(name, [P, S], U32)
+            nc.vector.tensor_copy(
+                dealt[:].bitcast(I32).rearrange("p (t c i) -> p c t i", t=PACK, i=4),
+                picked[:].bitcast(I32).rearrange("p (c i t) -> p c t i", t=PACK, i=4),
+            )
+            return dealt
+
+        def deal_bytes(name, picked):
+            dealt = new(name, [P, S], U8)
+            nc.vector.tensor_copy(
+                dealt[:].rearrange("p (t c i) -> p c t i", t=PACK, i=16),
+                picked[:].rearrange("p (c i t) -> p c t i", t=PACK, i=16),
+            )
+            return dealt
+
+        def coded_scales(name, lst, tag):
+            dealt = deal_bytes(name, pick(name + "_picked", ds, lst, U8, tag))
+            rows = dealt[:].bitcast(I32)
+            for e in range(2):
+                nc.sync.dma_start(rows[2 + e : P : 32, :], rows[16 + e : P : 32, :])
+            return dealt
+
+        def product(out, w, w_scales, t, m, m_scales):
+            cols = slice(t * P, (t + 1) * P)
+            nc.tensor.matmul_mx(
+                out=out,
+                lhsT=w[:, cols].bitcast(FP8X4),
+                lhsT_scale=w_scales[:, cols],
+                rhs=m.bitcast(FP8X4),
+                rhs_scale=m_scales,
+                start=True,
+                stop=True,
+            )
+
+        def look_up(out, window, lst, hf, scale):
+            nc.scalar.activation(out, window[:].indirect(half_list(lst, hf)), ACT.Copy, scale=scale)
+
+        k1_s = coded_scales("k1_s", k1_l, "stage0")
+        offs_w = pick("offs_w", xw, offs_l, U32, "token_w")
+        offs_s = pick("offs_s", xs, offs_l, U8, "token_s")
+        k1_w = deal_words("k1_w", pick("k1_picked", dw, k1_l, U32, "stage1"))
+        h_ps = [ps.tile([P, S], F32, name=f"h_ps{t}", tag=f"left{t}") for t in range(PACK)]
+        for t in range(PACK):
+            product(h_ps[t][:], k1_w, k1_s, t, offs_w[:], offs_s[:])
+
+        k2_s = coded_scales("k2_s", k2_l, "stage1")
+        two_w = pick("two_w", xw, two_l, U32, "token_w")
+        two_s = pick("two_s", xs, two_l, U8, "token_s")
+        k2_w = deal_words("k2_w", pick("k2_picked", dw, k2_l, U32, "stage1"))
+        b_ps = [ps.tile([P, S], F32, name=f"b_ps{t}", tag=f"right{t}") for t in range(PACK)]
+        for t in range(PACK):
+            product(b_ps[t][:], k2_w, k2_s, t, two_w[:], two_s[:])
+
+        h = [new(f"h{t}", [P, S], F32) for t in range(PACK)]
+        z_w = new("z_w", [P, S], U32)
+        z_s = new("z_s", [P, S], U8)
+
+        def z_half(hf):
+            cols = half_cols(hf)
+            h1 = new(f"h1_{hf}", [P, PACK, HALF], F32)
+            h2 = new(f"h2_{hf}", [P, PACK, HALF], F32)
+            pa = new(f"pa_{hf}", [P, PACK, HALF], F32)
+            pb = new(f"pb_{hf}", [P, PACK, HALF], F32)
+            low = new(f"low_{hf}", [P, PACK, HALF], F32)
+            pairs = new(f"pairs_{hf}", [P, 2, HALF, 2], BF16)
+            grouped = new(f"grouped_{hf}", [P, HALF, PACK], BF16)
+            for u in range(2):
+                for t in (2 * u, 2 * u + 1):
+                    if hf == 0:
+                        nc.scalar.activation(h[t][:], h_ps[t][:], ACT.Copy, scale=gain16[:, t : t + 1])
+                    look_up(h1[:, t, :], h[t], n1_l, hf, 1.0)
+                    look_up(h2[:, t, :], h[t], n2_l, hf, 1.0)
+                    nc.vector.tensor_tensor(pa[:, t, :], h[t][:, cols], h1[:, t, :], ALU.subtract)
+                    nc.vector.tensor_tensor(pb[:, t, :], h2[:, t, :], h[t][:, cols], ALU.subtract)
+                ts = slice(2 * u, 2 * u + 2)
+                nc.vector.scalar_tensor_tensor(low[:, ts, :], pb[:, ts, :], 0.0, pa[:, ts, :], ALU.max, ALU.min)
+                nc.vector.scalar_tensor_tensor(
+                    pairs[:, u, :, :],
+                    pb[:, ts, :].rearrange("p e j -> p j e"),
+                    0.0,
+                    low[:, ts, :].rearrange("p e j -> p j e"),
+                    ALU.min,
+                    ALU.max,
+                )
+            nc.vector.tensor_copy(
+                grouped[:].rearrange("p j r -> p (j r)").bitcast(F32).rearrange("p (j u) -> p j u", u=2),
+                pairs[:].rearrange("p u j e -> p (u j e)").bitcast(F32).rearrange("p (u j) -> p j u", u=2),
+            )
+            nc.vector.quantize_mx(
+                out=z_w[:, cols].bitcast(FP8X4), scales=z_s[:, cols], in_=grouped[:].rearrange("p j r -> p (j r)")
+            )
+
+        z_half(0)
+        cand_w = deal_words("cand_w", pick("cand_picked", xw, cand_l, U32, "stage1"))
+        cand_s = deal_bytes("cand_s", pick("cand_s_picked", xs, cand_l, U8, "stage1"))
+        a_ps = {}
+
+        def a_half(hf):
+            for u in range(2):
+                bank = ps.tile([P, 2, HALF], F32, name=f"a_ps{hf}{u}", tag=f"left{2 * hf + u}")
+                for e in range(2):
+                    product(bank[:, e, :], cand_w, cand_s, 2 * u + e, z_w[:, half_cols(hf)], z_s[:, half_cols(hf)])
+                    a_ps[2 * u + e, hf] = bank[:, e, :]
+
+        a_half(0)
+        z_half(1)
+
+        tau = []
+        for t in range(PACK):
+            b = new(f"b{t}", [P, S], F32)
+            b4 = new(f"b4_{t}", [P, S], F32)
+            nc.scalar.activation(b[:], b_ps[t][:], ACT.Copy, scale=SIXTEENTH)
+            for hf in range(2):
+                look_up(b4[:, half_cols(hf)], b, n4_l, hf, -1.0)
+            diff = ps.tile([P, S], F32, name=f"diff{t}", tag=f"right{t}")
+            for c in range(S // P):
+                cols = slice(c * P, (c + 1) * P)
+                nc.tensor.matmul(diff[:, cols], b[:, cols], ident[:], start=True, stop=False, is_transpose=True)
+                nc.tensor.matmul(diff[:, cols], b4[:, cols], ident[:], start=False, stop=True, is_transpose=True)
+            turned = new(f"turned{t}", [P, S], F32)
+            nc.scalar.activation(turned[:], diff[:], ACT.Tanh, scale=-0.5)
+            back = ps.tile([P, S], F32, name=f"tau{t}", tag=f"right{t}")
+            for c in range(S // P):
+                cols = slice(c * P, (c + 1) * P)
+                nc.tensor.transpose(back[:, cols], turned[:, cols], ident[:])
+            tau.append(back)
+
+        a_half(1)
+
+        a = [new(f"a{t}", [P, S], F32) for t in range(PACK)]
+        stay = [new(f"stay{hf}", [P, PACK, HALF], F32) for hf in range(2)]
+        for hf in range(2):
+            cols = half_cols(hf)
+            for t in range(PACK):
+                nc.scalar.activation(a[t][:, cols], a_ps[t, hf], ACT.Copy, scale=SIXTEENTH / 2)
+                nc.vector.scalar_tensor_tensor(
+                    stay[hf][:, t, :], tau[t][:, cols], 1.0, a[t][:, cols], ALU.subtract, ALU.mult
+                )
+
+        y_w = new("y_w", [P, S], U32)
+        y_s = new("y_s", [P, S], U8)
+        out_rows = out_0.rearrange("(p t) c -> p t c", t=PACK)
+        out_words = out_1[0].rearrange("p c r -> p (c r)").bitcast(I32)
+        for hf in range(2):
+            cols = half_cols(hf)
+            a3 = new(f"a3_{hf}", [P, PACK, HALF], F32)
+            come = new(f"come{hf}", [P, PACK, HALF], F32)
+            y = new(f"y{hf}", [P, PACK, HALF], F32)
+            y16 = new(f"y16_{hf}", [P, HALF, PACK], BF16)
+            for u in range(2):
+                ts = slice(2 * u, 2 * u + 2)
+                for t in (2 * u, 2 * u + 1):
+                    look_up(a3[:, t, :], a[t], n3_l, hf, 1.0)
+                    nc.vector.scalar_tensor_tensor(
+                        come[:, t, :], tau[t][:, cols], 1.0, a3[:, t, :], ALU.add, ALU.mult
+                    )
+                nc.vector.tensor_tensor(y[:, ts, :], come[:, ts, :], stay[hf][:, ts, :], ALU.subtract)
+                nc.sync.dma_start(out_rows[:, ts, cols], y[:, ts, :])
+            grouped_view = y16[:].rearrange("p (c i) t -> p c t i", i=4)
+            planes_view = y[:].rearrange("p t (c i) -> p c t i", i=4)
+            nc.vector.tensor_copy(grouped_view, planes_view)
+            nc.vector.quantize_mx(
+                out=y_w[:, cols].bitcast(FP8X4), scales=y_s[:, cols], in_=y16[:].rearrange("p j r -> p (j r)")
+            )
+            nc.sync.dma_start(out_words[:, cols], y_w[:, cols].bitcast(I32))
+        y_rows = y_s[:].bitcast(I32)
+        out_scales = out_2[0].bitcast(I32)
+        for q in range(4):
+            queue = nc.sync if q % 2 == 0 else nc.scalar
+            queue.dma_start(out_scales[4 * q : 4 * q + 4, :], y_rows[32 * q : 32 * q + 4, :])

@@ -49,26 +49,26 @@ def tile_picked_pqcjpullbminmod_none_po_kernel(
         dw = new("dw", [P, G], U32)
         xs = new("xs", [P, T], U8)
         ds = new("ds", [P, G], U8)
-        nc.vector.memset(ds[:].bitcast(I32), 0)
-        nc.gpsimd.memset(xs[:].bitcast(I32), 0)
+        nc.gpsimd.memset(ds[:].bitcast(I32), 0)
+        nc.vector.memset(xs[:].bitcast(I32), 0)
 
+        offs_l = load_list("offs_l", offs)
+        nc.sync.dma_start(xw[:].bitcast(I32), x_words[0].rearrange("p n r -> p (n r)").bitcast(I32))
         k1_l = load_list("k1_l", k1)
         ds32 = ds[:].bitcast(I32)
         d_rows = d_scales[0].bitcast(I32)
         for e in range(2):
             nc.sync.dma_start(ds32[e:P:16, :], d_rows[e:16:2, :])
-        offs_l = load_list("offs_l", offs)
-        nc.sync.dma_start(xw[:].bitcast(I32), x_words[0].rearrange("p n r -> p (n r)").bitcast(I32))
+        nc.sync.dma_start(dw[:].bitcast(I32), d_words[0].rearrange("p n r -> p (n r)").bitcast(I32))
         xs32 = xs[:].bitcast(I32)
         x_rows = x_scales[0].bitcast(I32)
         for q in range(4):
-            nc.scalar.dma_start(xs32[32 * q : 32 * q + 4, :], x_rows[4 * q : 4 * q + 4, :])
-        nc.sync.dma_start(dw[:].bitcast(I32), d_words[0].rearrange("p n r -> p (n r)").bitcast(I32))
+            nc.sync.dma_start(xs32[32 * q : 32 * q + 4, :], x_rows[4 * q : 4 * q + 4, :])
         gain = new("gain", [P, PACK], F32)
-        nc.scalar.dma_start(gain[:], gs.rearrange("(p t) o -> p (t o)", t=PACK))
-        k2_l = load_list("k2_l", k2)
+        nc.sync.dma_start(gain[:], gs.rearrange("(p t) o -> p (t o)", t=PACK))
         n1_l = load_list("n1_l", n1)
         n2_l = load_list("n2_l", n2)
+        k2_l = load_list("k2_l", k2)
         two_l = load_list("two_l", two)
         cand_l = load_list("cand_l", cand)
         n4_l = load_list("n4_l", n4)
@@ -100,11 +100,11 @@ def tile_picked_pqcjpullbminmod_none_po_kernel(
             )
             return dealt
 
-        def coded_scales(name, lst, tag):
+        def coded_scales(name, lst, tag, queue):
             dealt = deal_bytes(name, pick(name + "_picked", ds, lst, U8, tag))
             rows = dealt[:].bitcast(I32)
             for e in range(2):
-                nc.sync.dma_start(rows[2 + e : P : 32, :], rows[16 + e : P : 32, :])
+                queue.dma_start(rows[2 + e : P : 32, :], rows[16 + e : P : 32, :])
             return dealt
 
         def product(out, w, w_scales, t, m, m_scales):
@@ -122,87 +122,79 @@ def tile_picked_pqcjpullbminmod_none_po_kernel(
         def look_up(out, window, lst, hf, scale):
             nc.scalar.activation(out, window[:].indirect(half_list(lst, hf)), ACT.Copy, scale=scale)
 
-        k1_s = coded_scales("k1_s", k1_l, "stage0")
         offs_w = pick("offs_w", xw, offs_l, U32, "token_w")
+        k1_s = coded_scales("k1_s", k1_l, "stage0", nc.scalar)
         offs_s = pick("offs_s", xs, offs_l, U8, "token_s")
         k1_w = deal_words("k1_w", pick("k1_picked", dw, k1_l, U32, "stage1"))
         h_ps = [ps.tile([P, S], F32, name=f"h_ps{t}", tag=f"left{t}") for t in range(PACK)]
         for t in range(PACK):
             product(h_ps[t][:], k1_w, k1_s, t, offs_w[:], offs_s[:])
+        h = [new(f"h{t}", [P, S], F32) for t in range(PACK)]
+        nc.scalar.activation(h[0][:], h_ps[0][:], ACT.Copy, scale=gain16[:, 0:1])
+        for t in range(1, PACK):
+            nc.vector.tensor_scalar(h[t][:], h_ps[t][:], gain16[:, t : t + 1], None, ALU.mult)
 
-        k2_s = coded_scales("k2_s", k2_l, "stage1")
+        k2_s = coded_scales("k2_s", k2_l, "stage1", nc.sync)
         two_w = pick("two_w", xw, two_l, U32, "token_w")
         two_s = pick("two_s", xs, two_l, U8, "token_s")
         k2_w = deal_words("k2_w", pick("k2_picked", dw, k2_l, U32, "stage1"))
         b_ps = [ps.tile([P, S], F32, name=f"b_ps{t}", tag=f"right{t}") for t in range(PACK)]
         for t in range(PACK):
             product(b_ps[t][:], k2_w, k2_s, t, two_w[:], two_s[:])
-
-        h = [new(f"h{t}", [P, S], F32) for t in range(PACK)]
-        z_w = new("z_w", [P, S], U32)
-        z_s = new("z_s", [P, S], U8)
-
-        def z_half(hf):
-            cols = half_cols(hf)
-            h1 = new(f"h1_{hf}", [P, PACK, HALF], F32)
-            h2 = new(f"h2_{hf}", [P, PACK, HALF], F32)
-            pa = new(f"pa_{hf}", [P, PACK, HALF], F32)
-            pb = new(f"pb_{hf}", [P, PACK, HALF], F32)
-            low = new(f"low_{hf}", [P, PACK, HALF], F32)
-            pairs = new(f"pairs_{hf}", [P, 2, HALF, 2], BF16)
-            grouped = new(f"grouped_{hf}", [P, HALF, PACK], BF16)
-            for u in range(2):
-                for t in (2 * u, 2 * u + 1):
-                    if hf == 0:
-                        nc.scalar.activation(h[t][:], h_ps[t][:], ACT.Copy, scale=gain16[:, t : t + 1])
-                    look_up(h1[:, t, :], h[t], n1_l, hf, 1.0)
-                    look_up(h2[:, t, :], h[t], n2_l, hf, 1.0)
-                    nc.vector.tensor_tensor(pa[:, t, :], h[t][:, cols], h1[:, t, :], ALU.subtract)
-                    nc.vector.tensor_tensor(pb[:, t, :], h2[:, t, :], h[t][:, cols], ALU.subtract)
-                ts = slice(2 * u, 2 * u + 2)
-                nc.vector.scalar_tensor_tensor(low[:, ts, :], pb[:, ts, :], 0.0, pa[:, ts, :], ALU.max, ALU.min)
-                nc.vector.scalar_tensor_tensor(
-                    pairs[:, u, :, :],
-                    pb[:, ts, :].rearrange("p e j -> p j e"),
-                    0.0,
-                    low[:, ts, :].rearrange("p e j -> p j e"),
-                    ALU.min,
-                    ALU.max,
-                )
-            nc.vector.tensor_copy(
-                grouped[:].rearrange("p j r -> p (j r)").bitcast(F32).rearrange("p (j u) -> p j u", u=2),
-                pairs[:].rearrange("p u j e -> p (u j e)").bitcast(F32).rearrange("p (u j) -> p j u", u=2),
-            )
-            nc.vector.quantize_mx(
-                out=z_w[:, cols].bitcast(FP8X4), scales=z_s[:, cols], in_=grouped[:].rearrange("p j r -> p (j r)")
-            )
-
-        z_half(0)
+        b = [new(f"b{t}", [P, S], F32) for t in range(PACK)]
         cand_w = deal_words("cand_w", pick("cand_picked", xw, cand_l, U32, "stage1"))
         cand_s = deal_bytes("cand_s", pick("cand_s_picked", xs, cand_l, U8, "stage1"))
-        a_ps = {}
 
-        def a_half(hf):
-            for u in range(2):
-                bank = ps.tile([P, 2, HALF], F32, name=f"a_ps{hf}{u}", tag=f"left{2 * hf + u}")
-                for e in range(2):
-                    product(bank[:, e, :], cand_w, cand_s, 2 * u + e, z_w[:, half_cols(hf)], z_s[:, half_cols(hf)])
-                    a_ps[2 * u + e, hf] = bank[:, e, :]
+        z_w = new("z_w", [P, S], U32)
+        z_s = new("z_s", [P, S], U8)
+        pa = new("pa", [P, PACK, S], F32)
+        pb = new("pb", [P, PACK, S], F32)
+        h1 = new("at_n1", [P, PACK, S], F32)
+        h2 = new("at_n2", [P, PACK, S], F32)
+        for t in range(PACK):
+            for hf in range(2):
+                look_up(h1[:, t, half_cols(hf)], h[t], n1_l, hf, 1.0)
+            nc.gpsimd.tensor_tensor(pa[:, t, :], h[t][:], h1[:, t, :], ALU.subtract)
+            for hf in range(2):
+                look_up(h2[:, t, half_cols(hf)], h[t], n2_l, hf, 1.0)
+            nc.gpsimd.tensor_tensor(pb[:, t, :], h2[:, t, :], h[t][:], ALU.subtract)
 
-        a_half(0)
-        z_half(1)
+        low = new("low", [P, PACK, S], F32)
+        pairs = new("pairs", [P, 2, S, 2], BF16)
+        grouped = new("grouped", [P, S, PACK], BF16)
+        for u in range(2):
+            ts = slice(2 * u, 2 * u + 2)
+            nc.vector.scalar_tensor_tensor(low[:, ts, :], pb[:, ts, :], 0.0, pa[:, ts, :], ALU.max, ALU.min)
+            nc.vector.scalar_tensor_tensor(
+                pairs[:, u, :, :],
+                pb[:, ts, :].rearrange("p e j -> p j e"),
+                0.0,
+                low[:, ts, :].rearrange("p e j -> p j e"),
+                ALU.min,
+                ALU.max,
+            )
+        nc.vector.tensor_copy(
+            grouped[:].rearrange("p j r -> p (j r)").bitcast(F32).rearrange("p (j u) -> p j u", u=2),
+            pairs[:].rearrange("p u j e -> p (u j e)").bitcast(F32).rearrange("p (u j) -> p j u", u=2),
+        )
+        nc.vector.quantize_mx(out=z_w[:].bitcast(FP8X4), scales=z_s[:], in_=grouped[:].rearrange("p j r -> p (j r)"))
+        a_ps = [ps.tile([P, S], F32, name=f"a_ps{t}", tag=f"left{t}") for t in range(PACK)]
+        for t in range(PACK):
+            product(a_ps[t][:], cand_w, cand_s, t, z_w[:], z_s[:])
 
         tau = []
         for t in range(PACK):
-            b = new(f"b{t}", [P, S], F32)
-            b4 = new(f"b4_{t}", [P, S], F32)
-            nc.scalar.activation(b[:], b_ps[t][:], ACT.Copy, scale=SIXTEENTH)
+            b4 = new(f"b4_{t}", [P, S], F32, f"fetched{t}")
+            if t < PACK - 1:
+                nc.scalar.activation(b[t][:], b_ps[t][:], ACT.Copy, scale=SIXTEENTH)
+            else:
+                nc.vector.tensor_scalar(b[t][:], b_ps[t][:], SIXTEENTH, None, ALU.mult)
             for hf in range(2):
-                look_up(b4[:, half_cols(hf)], b, n4_l, hf, -1.0)
+                look_up(b4[:, half_cols(hf)], b[t], n4_l, hf, -1.0)
             diff = ps.tile([P, S], F32, name=f"diff{t}", tag=f"right{t}")
             for c in range(S // P):
                 cols = slice(c * P, (c + 1) * P)
-                nc.tensor.matmul(diff[:, cols], b[:, cols], ident[:], start=True, stop=False, is_transpose=True)
+                nc.tensor.matmul(diff[:, cols], b[t][:, cols], ident[:], start=True, stop=False, is_transpose=True)
                 nc.tensor.matmul(diff[:, cols], b4[:, cols], ident[:], start=False, stop=True, is_transpose=True)
             turned = new(f"turned{t}", [P, S], F32)
             nc.scalar.activation(turned[:], diff[:], ACT.Tanh, scale=-0.5)
@@ -212,25 +204,21 @@ def tile_picked_pqcjpullbminmod_none_po_kernel(
                 nc.tensor.transpose(back[:, cols], turned[:, cols], ident[:])
             tau.append(back)
 
-        a_half(1)
-
         a = [new(f"a{t}", [P, S], F32) for t in range(PACK)]
-        stay = [new(f"stay{hf}", [P, PACK, HALF], F32) for hf in range(2)]
-        for hf in range(2):
-            cols = half_cols(hf)
-            for t in range(PACK):
-                nc.scalar.activation(a[t][:, cols], a_ps[t, hf], ACT.Copy, scale=SIXTEENTH / 2)
-                nc.vector.scalar_tensor_tensor(
-                    stay[hf][:, t, :], tau[t][:, cols], 1.0, a[t][:, cols], ALU.subtract, ALU.mult
-                )
+        stay = new("stay", [P, PACK, S], F32)
+        for t in range(PACK):
+            nc.vector.tensor_scalar(a[t][:], a_ps[t][:], SIXTEENTH / 2, None, ALU.mult)
+        for t in range(PACK):
+            nc.vector.scalar_tensor_tensor(stay[:, t, :], tau[t][:], 1.0, a[t][:], ALU.subtract, ALU.mult)
 
         y_w = new("y_w", [P, S], U32)
         y_s = new("y_s", [P, S], U8)
         out_rows = out_0.rearrange("(p t) c -> p t c", t=PACK)
         out_words = out_1[0].rearrange("p c r -> p (c r)").bitcast(I32)
+        at_n3 = new("at_n3", [P, 2, PACK, HALF], F32, f"fetched{PACK - 1}")
         for hf in range(2):
             cols = half_cols(hf)
-            a3 = new(f"a3_{hf}", [P, PACK, HALF], F32)
+            a3 = at_n3[:, hf]
             come = new(f"come{hf}", [P, PACK, HALF], F32)
             y = new(f"y{hf}", [P, PACK, HALF], F32)
             y16 = new(f"y16_{hf}", [P, HALF, PACK], BF16)
@@ -241,7 +229,8 @@ def tile_picked_pqcjpullbminmod_none_po_kernel(
                     nc.vector.scalar_tensor_tensor(
                         come[:, t, :], tau[t][:, cols], 1.0, a3[:, t, :], ALU.add, ALU.mult
                     )
-                nc.vector.tensor_tensor(y[:, ts, :], come[:, ts, :], stay[hf][:, ts, :], ALU.subtract)
+                engine = nc.vector if (hf, u) == (1, 1) else nc.gpsimd
+                engine.tensor_tensor(y[:, ts, :], come[:, ts, :], stay[:, ts, cols], ALU.subtract)
                 nc.sync.dma_start(out_rows[:, ts, cols], y[:, ts, :])
             grouped_view = y16[:].rearrange("p (c i) t -> p c t i", i=4)
             planes_view = y[:].rearrange("p t (c i) -> p c t i", i=4)

@@ -130,20 +130,19 @@ def tile_picked_pqcjpullbminmod_none_po_kernel(
         for t in range(PACK):
             product(h_ps[t][:], k1_w, k1_s, t, offs_w[:], offs_s[:])
         h = [new(f"h{t}", [P, S], F32) for t in range(PACK)]
-        nc.scalar.activation(h[0][:], h_ps[0][:], ACT.Copy, scale=gain16[:, 0:1])
-        for t in range(1, PACK):
-            nc.vector.tensor_scalar(h[t][:], h_ps[t][:], gain16[:, t : t + 1], None, ALU.mult)
+        for t in range(PACK - 1):
+            nc.scalar.activation(h[t][:], h_ps[t][:], ACT.Copy, scale=gain16[:, t : t + 1])
+        nc.vector.tensor_scalar(h[PACK - 1][:], h_ps[PACK - 1][:], gain16[:, PACK - 1 : PACK], None, ALU.mult)
 
         k2_s = coded_scales("k2_s", k2_l, "stage1", nc.sync)
         two_w = pick("two_w", xw, two_l, U32, "token_w")
         two_s = pick("two_s", xs, two_l, U8, "token_s")
-        k2_w = deal_words("k2_w", pick("k2_picked", dw, k2_l, U32, "stage1"))
+        k2_w = deal_words("k2_w", pick("k2_picked", dw, k2_l, U32, "k1_w"))
         b_ps = [ps.tile([P, S], F32, name=f"b_ps{t}", tag=f"right{t}") for t in range(PACK)]
         for t in range(PACK):
             product(b_ps[t][:], k2_w, k2_s, t, two_w[:], two_s[:])
-        b = [new(f"b{t}", [P, S], F32) for t in range(PACK)]
-        cand_w = deal_words("cand_w", pick("cand_picked", xw, cand_l, U32, "stage1"))
-        cand_s = deal_bytes("cand_s", pick("cand_s_picked", xs, cand_l, U8, "stage1"))
+        cand_w = deal_words("cand_w", pick("cand_picked", xw, cand_l, U32, "k1_s"))
+        cand_s = deal_bytes("cand_s", pick("cand_s_picked", xs, cand_l, U8, "k1_w"))
 
         z_w = new("z_w", [P, S], U32)
         z_s = new("z_s", [P, S], U8)
@@ -154,10 +153,10 @@ def tile_picked_pqcjpullbminmod_none_po_kernel(
         for t in range(PACK):
             for hf in range(2):
                 look_up(h1[:, t, half_cols(hf)], h[t], n1_l, hf, 1.0)
-            nc.gpsimd.tensor_tensor(pa[:, t, :], h[t][:], h1[:, t, :], ALU.subtract)
+            nc.vector.tensor_tensor(pa[:, t, :], h[t][:], h1[:, t, :], ALU.subtract)
             for hf in range(2):
                 look_up(h2[:, t, half_cols(hf)], h[t], n2_l, hf, 1.0)
-            nc.gpsimd.tensor_tensor(pb[:, t, :], h2[:, t, :], h[t][:], ALU.subtract)
+            nc.vector.tensor_tensor(pb[:, t, :], h2[:, t, :], h[t][:], ALU.subtract)
 
         low = new("low", [P, PACK, S], F32)
         pairs = new("pairs", [P, 2, S, 2], BF16)
@@ -182,61 +181,76 @@ def tile_picked_pqcjpullbminmod_none_po_kernel(
         for t in range(PACK):
             product(a_ps[t][:], cand_w, cand_s, t, z_w[:], z_s[:])
 
-        tau = []
-        for t in range(PACK):
-            b4 = new(f"b4_{t}", [P, S], F32, f"fetched{t}")
-            if t < PACK - 1:
-                nc.scalar.activation(b[t][:], b_ps[t][:], ACT.Copy, scale=SIXTEENTH)
-            else:
-                nc.vector.tensor_scalar(b[t][:], b_ps[t][:], SIXTEENTH, None, ALU.mult)
-            for hf in range(2):
-                look_up(b4[:, half_cols(hf)], b[t], n4_l, hf, -1.0)
-            diff = ps.tile([P, S], F32, name=f"diff{t}", tag=f"right{t}")
-            for c in range(S // P):
-                cols = slice(c * P, (c + 1) * P)
-                nc.tensor.matmul(diff[:, cols], b[t][:, cols], ident[:], start=True, stop=False, is_transpose=True)
-                nc.tensor.matmul(diff[:, cols], b4[:, cols], ident[:], start=False, stop=True, is_transpose=True)
-            turned = new(f"turned{t}", [P, S], F32)
-            nc.scalar.activation(turned[:], diff[:], ACT.Tanh, scale=-0.5)
-            back = ps.tile([P, S], F32, name=f"tau{t}", tag=f"right{t}")
-            for c in range(S // P):
-                cols = slice(c * P, (c + 1) * P)
-                nc.tensor.transpose(back[:, cols], turned[:, cols], ident[:])
-            tau.append(back)
+        blocks = [slice(c * P, (c + 1) * P) for c in range(S // P)]
+        diff, tau, a, at_n3 = {}, {}, {}, {}
 
-        a = [new(f"a{t}", [P, S], F32) for t in range(PACK)]
-        stay = new("stay", [P, PACK, S], F32)
-        for t in range(PACK):
-            nc.vector.tensor_scalar(a[t][:], a_ps[t][:], SIXTEENTH / 2, None, ALU.mult)
-        for t in range(PACK):
-            nc.vector.scalar_tensor_tensor(stay[:, t, :], tau[t][:], 1.0, a[t][:], ALU.subtract, ALU.mult)
+        def fetch_b(t, tag=""):
+            b = new(f"b{t}", [P, S], F32, tag)
+            at_n4 = new(f"at_n4_{t}", [P, S], F32)
+            nc.scalar.activation(b[:], b_ps[t][:], ACT.Copy, scale=SIXTEENTH)
+            for hf in range(2):
+                look_up(at_n4[:, half_cols(hf)], b, n4_l, hf, -1.0)
+            diff[t] = ps.tile([P, S], F32, name=f"diff{t}", tag=f"right{t}")
+            for cols in blocks:
+                nc.tensor.matmul(diff[t][:, cols], b[:, cols], ident[:], start=True, stop=False, is_transpose=True)
+                nc.tensor.matmul(diff[t][:, cols], at_n4[:, cols], ident[:], start=False, stop=True, is_transpose=True)
+
+        def gate(t):
+            turned = new(f"turned{t}", [P, S], F32)
+            nc.scalar.activation(turned[:], diff[t][:], ACT.Tanh, scale=-0.5)
+            tau[t] = ps.tile([P, S], F32, name=f"tau{t}", tag=f"right{t}")
+            for cols in blocks:
+                nc.tensor.transpose(tau[t][:, cols], turned[:, cols], ident[:])
+
+        def fetch_a(t):
+            a[t] = new(f"a{t}", [P, S], F32)
+            at_n3[t] = new(f"at_n3_{t}", [P, S], F32)
+            if t < 2:
+                nc.vector.tensor_scalar(a[t][:], a_ps[t][:], SIXTEENTH / 2, None, ALU.mult)
+            else:
+                nc.scalar.activation(a[t][:], a_ps[t][:], ACT.Copy, scale=SIXTEENTH / 2)
+            for hf in range(2):
+                look_up(at_n3[t][:, half_cols(hf)], a[t], n3_l, hf, 1.0)
+
+        y = new("y", [P, PACK, S], F32)
+        out_rows = out_0.rearrange("(p t) c -> p t c", t=PACK)
+
+        def mix(t, pieces):
+            stay = new(f"stay{t}", [P, S], F32)
+            come = new(f"come{t}", [P, S], F32)
+            nc.vector.scalar_tensor_tensor(stay[:], tau[t][:], 1.0, a[t][:], ALU.subtract, ALU.mult)
+            for cols in pieces:
+                nc.vector.scalar_tensor_tensor(come[:, cols], tau[t][:, cols], 1.0, at_n3[t][:, cols], ALU.add, ALU.mult)
+                nc.vector.tensor_tensor(y[:, t, cols], come[:, cols], stay[:, cols], ALU.subtract)
+            nc.sync.dma_start(out_rows[:, t, :], y[:, t, :])
+
+        for t in range(3):
+            fetch_b(t)
+        for t in range(3):
+            gate(t)
+        fetch_a(0)
+        fetch_b(3, "pairs")
+        fetch_a(1)
+        gate(3)
+        fetch_a(2)
+        fetch_a(3)
+        for t in range(3):
+            mix(t, [slice(0, S)])
+        mix(3, [half_cols(0), half_cols(1)])
 
         y_w = new("y_w", [P, S], U32)
         y_s = new("y_s", [P, S], U8)
-        out_rows = out_0.rearrange("(p t) c -> p t c", t=PACK)
         out_words = out_1[0].rearrange("p c r -> p (c r)").bitcast(I32)
-        at_n3 = new("at_n3", [P, 2, PACK, HALF], F32, f"fetched{PACK - 1}")
-        for hf in range(2):
+        y16 = [new(f"y16_{hf}", [P, HALF, PACK], BF16) for hf in range(2)]
+        for hf, copy in ((0, nc.scalar.copy), (1, nc.vector.tensor_copy)):
+            copy(
+                y16[hf][:].rearrange("p (c i) t -> p c t i", i=4),
+                y[:, :, half_cols(hf)].rearrange("p t (c i) -> p c t i", i=4),
+            )
+        for hf in (1, 0):
             cols = half_cols(hf)
-            a3 = at_n3[:, hf]
-            come = new(f"come{hf}", [P, PACK, HALF], F32)
-            y = new(f"y{hf}", [P, PACK, HALF], F32)
-            y16 = new(f"y16_{hf}", [P, HALF, PACK], BF16)
-            for u in range(2):
-                ts = slice(2 * u, 2 * u + 2)
-                for t in (2 * u, 2 * u + 1):
-                    look_up(a3[:, t, :], a[t], n3_l, hf, 1.0)
-                    nc.vector.scalar_tensor_tensor(
-                        come[:, t, :], tau[t][:, cols], 1.0, a3[:, t, :], ALU.add, ALU.mult
-                    )
-                engine = nc.vector if (hf, u) == (1, 1) else nc.gpsimd
-                engine.tensor_tensor(y[:, ts, :], come[:, ts, :], stay[:, ts, cols], ALU.subtract)
-                nc.sync.dma_start(out_rows[:, ts, cols], y[:, ts, :])
-            grouped_view = y16[:].rearrange("p (c i) t -> p c t i", i=4)
-            planes_view = y[:].rearrange("p t (c i) -> p c t i", i=4)
-            nc.vector.tensor_copy(grouped_view, planes_view)
             nc.vector.quantize_mx(
-                out=y_w[:, cols].bitcast(FP8X4), scales=y_s[:, cols], in_=y16[:].rearrange("p j r -> p (j r)")
+                out=y_w[:, cols].bitcast(FP8X4), scales=y_s[:, cols], in_=y16[hf][:].rearrange("p j r -> p (j r)")
             )
             nc.sync.dma_start(out_words[:, cols], y_w[:, cols].bitcast(I32))
         y_rows = y_s[:].bitcast(I32)

@@ -78,6 +78,8 @@ def tile_picked_pqcjpullbminmod_none_po_kernel(
         make_identity(nc, ident[:])
         gain16 = new("gain16", [P, PACK], F32)
         nc.scalar.activation(gain16[:], gain[:], ACT.Copy, scale=SIXTEENTH)
+        minus16 = new("minus16", [P, PACK], F32)
+        nc.scalar.activation(minus16[:], gain[:], ACT.Copy, scale=-SIXTEENTH)
 
         def pick(name, table, lst, dtype, tag=""):
             picked = new(name, [P, S], dtype, tag)
@@ -130,9 +132,9 @@ def tile_picked_pqcjpullbminmod_none_po_kernel(
         for t in range(PACK):
             product(h_ps[t][:], k1_w, k1_s, t, offs_w[:], offs_s[:])
         h = [new(f"h{t}", [P, S], F32) for t in range(PACK)]
-        for t in range(PACK - 1):
-            nc.scalar.activation(h[t][:], h_ps[t][:], ACT.Copy, scale=gain16[:, t : t + 1])
-        nc.vector.tensor_scalar(h[PACK - 1][:], h_ps[PACK - 1][:], gain16[:, PACK - 1 : PACK], None, ALU.mult)
+        nc.scalar.activation(h[0][:], h_ps[0][:], ACT.Copy, scale=gain16[:, 0:1])
+        for t in range(1, PACK):
+            nc.vector.tensor_scalar(h[t][:], h_ps[t][:], gain16[:, t : t + 1], None, ALU.mult)
 
         k2_s = coded_scales("k2_s", k2_l, "stage1", nc.sync)
         two_w = pick("two_w", xw, two_l, U32, "token_w")
@@ -146,27 +148,32 @@ def tile_picked_pqcjpullbminmod_none_po_kernel(
 
         z_w = new("z_w", [P, S], U32)
         z_s = new("z_s", [P, S], U8)
-        pa = new("pa", [P, PACK, S], F32)
-        pb = new("pb", [P, PACK, S], F32)
+        steps = [new("steps0", [P, 2, 2, S], F32), new("steps1", [P, 2, 2, S], F32, "k1_w")]
         h1 = new("at_n1", [P, PACK, S], F32)
         h2 = new("at_n2", [P, PACK, S], F32)
         for t in range(PACK):
+            pa, pb = steps[t // 2][:, 0, t % 2, :], steps[t // 2][:, 1, t % 2, :]
             for hf in range(2):
                 look_up(h1[:, t, half_cols(hf)], h[t], n1_l, hf, 1.0)
-            nc.vector.tensor_tensor(pa[:, t, :], h[t][:], h1[:, t, :], ALU.subtract)
             for hf in range(2):
                 look_up(h2[:, t, half_cols(hf)], h[t], n2_l, hf, 1.0)
-            nc.vector.tensor_tensor(pb[:, t, :], h2[:, t, :], h[t][:], ALU.subtract)
+            if t == 2:
+                nc.gpsimd.tensor_tensor(pa, h[t][:], h1[:, t, :], ALU.subtract)
+                nc.gpsimd.tensor_tensor(pb, h2[:, t, :], h[t][:], ALU.subtract)
+            else:
+                nc.vector.scalar_tensor_tensor(pa, h_ps[t][:], gain16[:, t : t + 1], h1[:, t, :], ALU.mult, ALU.subtract)
+                nc.vector.scalar_tensor_tensor(pb, h_ps[t][:], minus16[:, t : t + 1], h2[:, t, :], ALU.mult, ALU.add)
 
         low = new("low", [P, PACK, S], F32)
         pairs = new("pairs", [P, 2, S, 2], BF16)
         grouped = new("grouped", [P, S, PACK], BF16)
         for u in range(2):
             ts = slice(2 * u, 2 * u + 2)
-            nc.vector.scalar_tensor_tensor(low[:, ts, :], pb[:, ts, :], 0.0, pa[:, ts, :], ALU.max, ALU.min)
+            pa, pb = steps[u][:, 0], steps[u][:, 1]
+            nc.vector.scalar_tensor_tensor(low[:, ts, :], pb, 0.0, pa, ALU.max, ALU.min)
             nc.vector.scalar_tensor_tensor(
                 pairs[:, u, :, :],
-                pb[:, ts, :].rearrange("p e j -> p j e"),
+                pb.rearrange("p e j -> p j e"),
                 0.0,
                 low[:, ts, :].rearrange("p e j -> p j e"),
                 ALU.min,
@@ -205,7 +212,7 @@ def tile_picked_pqcjpullbminmod_none_po_kernel(
         def fetch_a(t):
             a[t] = new(f"a{t}", [P, S], F32)
             at_n3[t] = new(f"at_n3_{t}", [P, S], F32)
-            if t < 2:
+            if t < 3:
                 nc.vector.tensor_scalar(a[t][:], a_ps[t][:], SIXTEENTH / 2, None, ALU.mult)
             else:
                 nc.scalar.activation(a[t][:], a_ps[t][:], ACT.Copy, scale=SIXTEENTH / 2)
@@ -221,7 +228,8 @@ def tile_picked_pqcjpullbminmod_none_po_kernel(
             nc.vector.scalar_tensor_tensor(stay[:], tau[t][:], 1.0, a[t][:], ALU.subtract, ALU.mult)
             for cols in pieces:
                 nc.vector.scalar_tensor_tensor(come[:, cols], tau[t][:, cols], 1.0, at_n3[t][:, cols], ALU.add, ALU.mult)
-                nc.vector.tensor_tensor(y[:, t, cols], come[:, cols], stay[:, cols], ALU.subtract)
+                engine = nc.gpsimd if t < 3 else nc.vector
+                engine.tensor_tensor(y[:, t, cols], come[:, cols], stay[:, cols], ALU.subtract)
             nc.sync.dma_start(out_rows[:, t, :], y[:, t, :])
 
         for t in range(3):

from contextlib import ExitStack

import concourse.mybir as mybir
from concourse.masks import make_identity

K, T, S, G = 512, 1024, 512, 2048
FLOPS = 3 * 2 * 512 * 512 * 512

F32 = mybir.dt.float32
BF16 = mybir.dt.bfloat16
I32 = mybir.dt.int32
U32 = mybir.dt.uint32
U16 = mybir.dt.uint16
U8 = mybir.dt.uint8
FP8X4 = mybir.dt.float8_e4m3fn_x4
ALU = mybir.AluOpType
ACT = mybir.ActivationFunctionType

P = 128
PACK = 4
HALF = S // 2
SIXTEENTH = 0.0625


def tile_picked_pqcjpullbminmod_none_po_kernel(
    tc, x_words, x_scales, d_words, d_scales, gs, offs, k1, n1, n2, cand, two, k2, n3, n4, out_0, out_1, out_2
):
    nc = tc.nc
    with ExitStack() as ctx:
        lists = ctx.enter_context(tc.tile_pool(name="lists", bufs=1))
        sb = ctx.enter_context(tc.tile_pool(name="sb", bufs=1))
        ps = ctx.enter_context(tc.psum_pool(name="ps", bufs=1))

        def new(name, shape, dtype, tag=""):
            return sb.tile(shape, dtype, name=name, tag=tag or name, align_bytes=64)

        def load_list(name, src):
            tile = lists.tile([P, S // 16], U16, name=name)
            nc.sync.dma_start(tile[:], src)
            return tile

        def half_cols(hf):
            return slice(hf * HALF, (hf + 1) * HALF)

        def half_list(lst, hf):
            return lst[:, hf * HALF // 16 : (hf + 1) * HALF // 16]

        xw = new("xw", [P, T], U32)
        dw = new("dw", [P, G], U32)
        xs = new("xs", [P, T], U8)
        ds = new("ds", [P, G], U8)
        nc.gpsimd.memset(ds[:].bitcast(I32), 0)
        nc.vector.memset(xs[:].bitcast(I32), 0)

        offs_l = load_list("offs_l", offs)
        nc.sync.dma_start(xw[:].bitcast(I32), x_words[0].rearrange("p n r -> p (n r)").bitcast(I32))
        k1_l = load_list("k1_l", k1)
        ds32 = ds[:].bitcast(I32)
        d_rows = d_scales[0].bitcast(I32)
        for e in range(2):
            nc.sync.dma_start(ds32[e:P:16, :], d_rows[e:16:2, :])
        nc.sync.dma_start(dw[:].bitcast(I32), d_words[0].rearrange("p n r -> p (n r)").bitcast(I32))
        xs32 = xs[:].bitcast(I32)
        x_rows = x_scales[0].bitcast(I32)
        for q in range(4):
            nc.sync.dma_start(xs32[32 * q : 32 * q + 4, :], x_rows[4 * q : 4 * q + 4, :])
        gain = new("gain", [P, PACK], F32)
        nc.sync.dma_start(gain[:], gs.rearrange("(p t) o -> p (t o)", t=PACK))
        n1_l = load_list("n1_l", n1)
        n2_l = load_list("n2_l", n2)
        k2_l = load_list("k2_l", k2)
        two_l = load_list("two_l", two)
        cand_l = load_list("cand_l", cand)
        n4_l = load_list("n4_l", n4)
        n3_l = load_list("n3_l", n3)

        ident = new("ident", [P, P], F32)
        make_identity(nc, ident[:])
        gain16 = new("gain16", [P, PACK], F32)
        nc.scalar.activation(gain16[:], gain[:], ACT.Copy, scale=SIXTEENTH)
        minus16 = new("minus16", [P, PACK], F32)
        nc.scalar.activation(minus16[:], gain[:], ACT.Copy, scale=-SIXTEENTH)

        def pick(name, table, lst, dtype, tag=""):
            picked = new(name, [P, S], dtype, tag)
            nc.vector.tensor_copy(picked[:], table[:].indirect(lst[:]))
            return picked

        def deal_words(name, picked):
            dealt = new(name, [P, S], U32)
            nc.vector.tensor_copy(
                dealt[:].bitcast(I32).rearrange("p (t c i) -> p c t i", t=PACK, i=4),
                picked[:].bitcast(I32).rearrange("p (c i t) -> p c t i", t=PACK, i=4),
            )
            return dealt

        def deal_bytes(name, picked):
            dealt = new(name, [P, S], U8)
            nc.vector.tensor_copy(
                dealt[:].rearrange("p (t c i) -> p c t i", t=PACK, i=16),
                picked[:].rearrange("p (c i t) -> p c t i", t=PACK, i=16),
            )
            return dealt

        def coded_scales(name, lst, tag, queue):
            dealt = deal_bytes(name, pick(name + "_picked", ds, lst, U8, tag))
            rows = dealt[:].bitcast(I32)
            for e in range(2):
                queue.dma_start(rows[2 + e : P : 32, :], rows[16 + e : P : 32, :])
            return dealt

        def product(out, w, w_scales, t, m, m_scales):
            cols = slice(t * P, (t + 1) * P)
            nc.tensor.matmul_mx(
                out=out,
                lhsT=w[:, cols].bitcast(FP8X4),
                lhsT_scale=w_scales[:, cols],
                rhs=m.bitcast(FP8X4),
                rhs_scale=m_scales,
                start=True,
                stop=True,
            )

        def look_up(out, window, lst, hf, scale):
            nc.scalar.activation(out, window[:].indirect(half_list(lst, hf)), ACT.Copy, scale=scale)

        offs_w = pick("offs_w", xw, offs_l, U32, "token_w")
        k1_s = coded_scales("k1_s", k1_l, "stage0", nc.scalar)
        offs_s = pick("offs_s", xs, offs_l, U8, "token_s")
        k1_w = deal_words("k1_w", pick("k1_picked", dw, k1_l, U32, "stage1"))
        h_ps = [ps.tile([P, S], F32, name=f"h_ps{t}", tag=f"left{t}") for t in range(PACK)]
        for t in range(PACK):
            product(h_ps[t][:], k1_w, k1_s, t, offs_w[:], offs_s[:])
        h = [new(f"h{t}", [P, S], F32) for t in range(PACK)]
        nc.scalar.activation(h[0][:], h_ps[0][:], ACT.Copy, scale=gain16[:, 0:1])
        for t in range(1, PACK):
            nc.vector.tensor_scalar(h[t][:], h_ps[t][:], gain16[:, t : t + 1], None, ALU.mult)

        k2_s = coded_scales("k2_s", k2_l, "stage1", nc.sync)
        two_w = pick("two_w", xw, two_l, U32, "token_w")
        two_s = pick("two_s", xs, two_l, U8, "token_s")
        k2_w = deal_words("k2_w", pick("k2_picked", dw, k2_l, U32, "k1_w"))
        b_ps = [ps.tile([P, S], F32, name=f"b_ps{t}", tag=f"right{t}") for t in range(PACK)]
        for t in range(PACK):
            product(b_ps[t][:], k2_w, k2_s, t, two_w[:], two_s[:])
        cand_w = deal_words("cand_w", pick("cand_picked", xw, cand_l, U32, "k1_s"))
        cand_s = deal_bytes("cand_s", pick("cand_s_picked", xs, cand_l, U8, "k1_w"))

        z_w = new("z_w", [P, S], U32)
        z_s = new("z_s", [P, S], U8)
        steps = [new("steps0", [P, 2, 2, S], F32), new("steps1", [P, 2, 2, S], F32, "k1_w")]
        h1 = new("at_n1", [P, PACK, S], F32)
        h2 = new("at_n2", [P, PACK, S], F32)
        for t in range(PACK):
            pa, pb = steps[t // 2][:, 0, t % 2, :], steps[t // 2][:, 1, t % 2, :]
            for hf in range(2):
                look_up(h1[:, t, half_cols(hf)], h[t], n1_l, hf, 1.0)
            for hf in range(2):
                look_up(h2[:, t, half_cols(hf)], h[t], n2_l, hf, 1.0)
            if t == 2:
                nc.gpsimd.tensor_tensor(pa, h[t][:], h1[:, t, :], ALU.subtract)
                nc.gpsimd.tensor_tensor(pb, h2[:, t, :], h[t][:], ALU.subtract)
            else:
                nc.vector.scalar_tensor_tensor(pa, h_ps[t][:], gain16[:, t : t + 1], h1[:, t, :], ALU.mult, ALU.subtract)
                nc.vector.scalar_tensor_tensor(pb, h_ps[t][:], minus16[:, t : t + 1], h2[:, t, :], ALU.mult, ALU.add)

        low = new("low", [P, PACK, S], F32)
        pairs = new("pairs", [P, 2, S, 2], BF16)
        grouped = new("grouped", [P, S, PACK], BF16)
        for u in range(2):
            ts = slice(2 * u, 2 * u + 2)
            pa, pb = steps[u][:, 0], steps[u][:, 1]
            nc.vector.scalar_tensor_tensor(low[:, ts, :], pb, 0.0, pa, ALU.max, ALU.min)
            nc.vector.scalar_tensor_tensor(
                pairs[:, u, :, :],
                pb.rearrange("p e j -> p j e"),
                0.0,
                low[:, ts, :].rearrange("p e j -> p j e"),
                ALU.min,
                ALU.max,
            )
        nc.vector.tensor_copy(
            grouped[:].rearrange("p j r -> p (j r)").bitcast(F32).rearrange("p (j u) -> p j u", u=2),
            pairs[:].rearrange("p u j e -> p (u j e)").bitcast(F32).rearrange("p (u j) -> p j u", u=2),
        )
        nc.vector.quantize_mx(out=z_w[:].bitcast(FP8X4), scales=z_s[:], in_=grouped[:].rearrange("p j r -> p (j r)"))
        a_ps = [ps.tile([P, S], F32, name=f"a_ps{t}", tag=f"left{t}") for t in range(PACK)]
        for t in range(PACK):
            product(a_ps[t][:], cand_w, cand_s, t, z_w[:], z_s[:])

        blocks = [slice(c * P, (c + 1) * P) for c in range(S // P)]
        diff, tau, a, at_n3 = {}, {}, {}, {}

        def fetch_b(t, tag=""):
            b = new(f"b{t}", [P, S], F32, tag)
            at_n4 = new(f"at_n4_{t}", [P, S], F32)
            nc.scalar.activation(b[:], b_ps[t][:], ACT.Copy, scale=SIXTEENTH)
            for hf in range(2):
                look_up(at_n4[:, half_cols(hf)], b, n4_l, hf, -1.0)
            diff[t] = ps.tile([P, S], F32, name=f"diff{t}", tag=f"right{t}")
            for cols in blocks:
                nc.tensor.matmul(diff[t][:, cols], b[:, cols], ident[:], start=True, stop=False, is_transpose=True)
                nc.tensor.matmul(diff[t][:, cols], at_n4[:, cols], ident[:], start=False, stop=True, is_transpose=True)

        def gate(t):
            turned = new(f"turned{t}", [P, S], F32)
            nc.scalar.activation(turned[:], diff[t][:], ACT.Tanh, scale=-0.5)
            tau[t] = ps.tile([P, S], F32, name=f"tau{t}", tag=f"right{t}")
            for cols in blocks:
                nc.tensor.transpose(tau[t][:, cols], turned[:, cols], ident[:])

        def fetch_a(t):
            a[t] = new(f"a{t}", [P, S], F32)
            at_n3[t] = new(f"at_n3_{t}", [P, S], F32)
            if t < 3:
                nc.vector.tensor_scalar(a[t][:], a_ps[t][:], SIXTEENTH / 2, None, ALU.mult)
            else:
                nc.scalar.activation(a[t][:], a_ps[t][:], ACT.Copy, scale=SIXTEENTH / 2)
            for hf in range(2):
                look_up(at_n3[t][:, half_cols(hf)], a[t], n3_l, hf, 1.0)

        y = new("y", [P, PACK, S], F32)
        out_rows = out_0.rearrange("(p t) c -> p t c", t=PACK)

        def mix(t, pieces):
            stay = new(f"stay{t}", [P, S], F32)
            come = new(f"come{t}", [P, S], F32)
            nc.vector.scalar_tensor_tensor(stay[:], tau[t][:], 1.0, a[t][:], ALU.subtract, ALU.mult)
            for cols in pieces:
                nc.vector.scalar_tensor_tensor(come[:, cols], tau[t][:, cols], 1.0, at_n3[t][:, cols], ALU.add, ALU.mult)
                engine = nc.gpsimd if t < 3 else nc.vector
                engine.tensor_tensor(y[:, t, cols], come[:, cols], stay[:, cols], ALU.subtract)
            nc.sync.dma_start(out_rows[:, t, :], y[:, t, :])

        for t in range(3):
            fetch_b(t)
        for t in range(3):
            gate(t)
        fetch_a(0)
        fetch_b(3, "pairs")
        fetch_a(1)
        gate(3)
        fetch_a(2)
        fetch_a(3)
        for t in range(3):
            mix(t, [slice(0, S)])
        mix(3, [half_cols(0), half_cols(1)])

        y_w = new("y_w", [P, S], U32)
        y_s = new("y_s", [P, S], U8)
        out_words = out_1[0].rearrange("p c r -> p (c r)").bitcast(I32)
        y16 = [new(f"y16_{hf}", [P, HALF, PACK], BF16) for hf in range(2)]
        for hf, copy in ((0, nc.scalar.copy), (1, nc.vector.tensor_copy)):
            copy(
                y16[hf][:].rearrange("p (c i) t -> p c t i", i=4),
                y[:, :, half_cols(hf)].rearrange("p t (c i) -> p c t i", i=4),
            )
        for hf in (1, 0):
            cols = half_cols(hf)
            nc.vector.quantize_mx(
                out=y_w[:, cols].bitcast(FP8X4), scales=y_s[:, cols], in_=y16[hf][:].rearrange("p j r -> p (j r)")
            )
            nc.sync.dma_start(out_words[:, cols], y_w[:, cols].bitcast(I32))
        y_rows = y_s[:].bitcast(I32)
        out_scales = out_2[0].bitcast(I32)
        for q in range(4):
            queue = nc.sync if q % 2 == 0 else nc.scalar
            queue.dma_start(out_scales[4 * q : 4 * q + 4, :], y_rows[32 * q : 32 * q + 4, :])
